import numpy as np
import ml_dtypes


def mxq(x, axis, fmt="e4m3"):
    dtype, down = {"e4m3": (ml_dtypes.float8_e4m3fn, 7), "e5m2": (ml_dtypes.float8_e5m2, 14)}[fmt]
    v = np.moveaxis(np.asarray(x, np.float32).astype(ml_dtypes.bfloat16).astype(np.float64), axis, -1)
    blocks = v.reshape(v.shape[:-1] + (-1, 32))
    amax = np.abs(blocks).max(-1, keepdims=True)
    byte = np.maximum(np.where(amax > 0, np.frexp(amax)[1] - 1 + 127, 0) - down, 1)
    scale = np.exp2(byte - 127.0)
    codes = (blocks / scale).astype(np.float32).astype(dtype).astype(np.float64)
    return np.moveaxis((codes * scale).reshape(v.shape), -1, axis)


WIDE = False


def mx_kscale(k):
    if not WIDE:
        return np.ones(k)
    levels = np.array([10, -10, 5, -5, 0])
    if k % 512:
        return np.exp2(np.random.permutation(np.resize(levels, k // 32))).repeat(32)
    a = np.empty((k // 512, 16))
    for p in range(k // 512):
        a[p, :8] = np.random.permutation(np.resize(levels, 8))
        for g in range(8):
            far = levels[np.abs(levels - a[p, g]) >= 10]
            a[p, g + 8] = far[np.random.randint(len(far))]
    return np.exp2(a.ravel()).repeat(32)


def f64(x):
    return np.asarray(x).astype(np.float64)


def striped(idx):
    return np.tile(idx.reshape(-1, 16).T, (8, 1)).astype(np.uint16)


def unstriped(offs):
    return offs[:16].T.reshape(-1).astype(np.int64)


def striped8(idx):
    return np.concatenate([x.reshape(-1, 16).T for x in idx]).astype(np.uint16)


def runs(offs, k):
    lists = np.stack([offs[16 * r : 16 * r + 16].T.reshape(-1) for r in range(8)]).astype(np.int64)
    return lists[np.arange(k) % 512 // 64]


def pack_weight(w):
    k, n = w.shape
    w = f64(np.asarray(w, np.float32).astype(ml_dtypes.bfloat16)).reshape(k // 32, 32, n)
    amax = np.abs(w).max(1)
    byte = np.clip(np.where(amax > 0, np.frexp(amax)[1] - 1 + 127 - 7, 1), 1, 254)
    scaled = (w * np.exp2(127.0 - byte)[:, None, :]).reshape(k, n).astype(np.float32)
    words = np.ascontiguousarray(scaled.reshape(k // 512, 128, 4, n).transpose(0, 1, 3, 2)).astype(ml_dtypes.float8_e4m3fn).view(np.uint8)
    return words, np.ascontiguousarray(byte.astype(np.uint8).reshape(k // 512, 16, n))


def unpack_weight(words, scales):
    g, p, n, _ = words.shape
    vals = np.ascontiguousarray(words).view(ml_dtypes.float8_e4m3fn).astype(np.float64) * np.repeat(np.exp2(scales.astype(np.float64) - 127.0), 8, axis=1)[..., None]
    return vals.transpose(0, 1, 3, 2).reshape(g * 512, n)


K, T, S, N, H, W, U = 512, 2048, 512, 512, 512, 256, 1024


def setup_inputs():
    n = np.random.standard_normal
    s = mx_kscale(K)[:, None]
    u = mx_kscale(S)
    packed_xT = pack_weight(n((K, T)) * s)
    perm = np.stack([np.random.permutation(H) for _ in range(8)])
    return {
        "x_words": packed_xT[0],
        "x_scales": packed_xT[1],
        "wa": (n((K, H)) / np.sqrt(K) / s).astype(np.float32),
        "wb": (n((K, N)) / np.sqrt(K) / s).astype(np.float32),
        "gt": (np.random.uniform(0.5, 1.5, (S, 1)) * u[:, None]).astype(np.float32),
        "gi": (np.random.uniform(0.5, 1.5, (S, 1)) / u[:, None]).astype(np.float32),
        "mem": n((H, U)).astype(np.float32),
        "offs": striped(np.random.permutation(T)[:S]),
        "two": striped(np.random.permutation(T)[:S]),
        "n1": striped8(perm[:, :W]),
        "n2": striped8(perm[:, W:]),
        "n3": striped8(np.stack([np.random.permutation(U)[:N] for _ in range(8)])),
    }


def reference(x_words, x_scales, wa, wb, gt, gi, mem, offs, two, n1, n2, n3):
    xq = unpack_weight(x_words, x_scales)[:, unstriped(offs)]
    a = xq.T @ mxq(f64(wa), 0, "e4m3")
    pa = a[np.arange(S)[:, None], runs(n1, S)]
    pb = a[np.arange(S)[:, None], runs(n2, S)]
    rb = pa * pb
    ra = pa + pb
    ds = np.zeros((S, H))
    ds[np.arange(S)[:, None], runs(n1, S)] = ra
    dt = ds.copy()
    dt[np.arange(S)[:, None], runs(n2, S)] = rb
    z = f64(gt) * dt
    x_two = unpack_weight(x_words, x_scales)[:, unstriped(two)]
    b = x_two.T @ mxq(f64(wb), 0, "e4m3")
    z2 = f64(gi) * b
    cv = 0.0625 * ((mxq(z, 0, "e4m3").T @ mxq(z2, 0, "e4m3")))
    nw = np.maximum(cv, 0.5 * (f64(mem)[np.arange(H)[:, None], runs(n3, H)]))
    out = f64(mem).copy()
    out[np.arange(H)[:, None], runs(n3, H)] = nw
    return out

@@ -1,0 +1,217 @@
+from contextlib import ExitStack
+
+import concourse.mybir as mybir
+from concourse.masks import make_identity
+
+K, T, S, N, H, W, U = 512, 2048, 512, 512, 512, 256, 1024
+FLOPS = 2 * K * S * H + 2 * K * S * N + 2 * S * H * N
+
+F32 = mybir.dt.float32
+BF16 = mybir.dt.bfloat16
+I32 = mybir.dt.int32
+U32 = mybir.dt.uint32
+U16 = mybir.dt.uint16
+U8 = mybir.dt.uint8
+FP8X4 = mybir.dt.float8_e4m3fn_x4
+COPY = mybir.ActivationFunctionType.Copy
+ADD = mybir.AluOpType.add
+MULT = mybir.AluOpType.mult
+MAX = mybir.AluOpType.max
+
+P = 128
+PACK = 4
+HALF = H // 2
+
+
+def tile_picked_mombondpagex_none_p_kernel(
+    tc, x_words, x_scales, wa, wb, gt, gi, mem, offs, two, n1, n2, n3, out
+):
+    nc = tc.nc
+    with ExitStack() as ctx:
+        keep = ctx.enter_context(tc.tile_pool(name="keep", bufs=1))
+        psum = ctx.enter_context(tc.psum_pool(name="psum", bufs=1))
+
+        def load_list(name, src):
+            lst = keep.tile(list(src.shape), U16, name=name)
+            nc.sync.dma_start(lst[:], src)
+            return lst
+
+        offs_sb = load_list("offs_sb", offs)
+        scale_tab = keep.tile([P, T], U8, name="scale_tab", align_bytes=64)
+        nc.gpsimd.memset(scale_tab[:].bitcast(I32), 0)
+        for q in range(4):
+            nc.scalar.dma_start(
+                scale_tab[32 * q : 32 * q + 4, :].bitcast(I32), x_scales[0, 4 * q : 4 * q + 4, :].bitcast(I32)
+            )
+        word_tab = keep.tile([P, T], U32, name="word_tab", align_bytes=64)
+        words_in = x_words[0].rearrange("p n t -> p (n t)").bitcast(I32)
+        for h in range(2):
+            cols = slice(h * T // 2, (h + 1) * T // 2)
+            nc.sync.dma_start(word_tab[:].bitcast(I32)[:, cols], words_in[:, cols])
+        two_sb = load_list("two_sb", two)
+
+        wa_rows = wa.rearrange("(p j) h -> p j h", j=PACK)
+        wa_raw = []
+        for h in range(2):
+            raw = keep.tile([P, PACK, HALF], F32, name=f"wa_raw{h}")
+            nc.sync.dma_start(raw[:], wa_rows[:, :, h * HALF : (h + 1) * HALF])
+            wa_raw.append(raw)
+        n1_sb = load_list("n1_sb", n1)
+        n2_sb = load_list("n2_sb", n2)
+        n3_sb = load_list("n3_sb", n3)
+        mem_rows = mem.rearrange("(p t) u -> t p u", t=PACK)
+        out_rows = out.rearrange("(p t) u -> t p u", t=PACK)
+        page = [keep.tile([P, U], F32, name=f"page{t}") for t in range(PACK)]
+        nc.sync.dma_start(page[0][:], mem_rows[0])
+        wb_raw = keep.tile([P, PACK, N], F32, name="wb_raw")
+        nc.sync.dma_start(wb_raw[:], wb.rearrange("(p j) n -> p j n", j=PACK))
+        for t in range(1, PACK):
+            nc.sync.dma_start(page[t][:], mem_rows[t])
+
+        gate_rows = keep.tile([P, P], F32, name="gate_rows")
+        ident = keep.tile([P, P], F32, name="ident")
+        nc.gpsimd.memset(gate_rows[:], 0.0)
+        make_identity(nc, ident[:])
+        for g, src in enumerate((gt, gi)):
+            nc.scalar.dma_start(
+                gate_rows[PACK * g : PACK * (g + 1), :].rearrange("t (b q) -> t b q", q=8),
+                src.rearrange("(b t q) o -> t b (q o)", t=PACK, q=8),
+            )
+        gate_ps = psum.tile([P, P], F32, name="gate_ps")
+        nc.tensor.transpose(gate_ps[:], gate_rows[:], ident[:])
+        gates = keep.tile([P, 2 * PACK], F32, name="gates")
+        nc.scalar.activation(gates[:], gate_ps[:, 0 : 2 * PACK], COPY)
+
+        picked_scales = keep.tile([P, 2 * S], U8, name="picked_scales", align_bytes=64)
+        nc.vector.tensor_copy(picked_scales[:, 0:S], scale_tab[:].indirect(offs_sb[:]))
+        nc.vector.tensor_copy(picked_scales[:, S : 2 * S], scale_tab[:].indirect(two_sb[:]))
+        xa = keep.tile([P, S], U32, name="xa", align_bytes=64)
+        xb = keep.tile([P, S], U32, name="xb", align_bytes=64)
+        nc.vector.tensor_copy(xa[:].rearrange("p (t b q) -> p b t q", t=PACK, q=8), word_tab[:].indirect(offs_sb[:]))
+        dealt_scales = keep.tile([P, 2 * S], U8, name="dealt_scales", align_bytes=64)
+        nc.vector.tensor_copy(
+            dealt_scales[:].bitcast(I32).rearrange("p (l t b e) -> p l t b e", l=2, t=PACK, e=2),
+            picked_scales[:].bitcast(I32).rearrange("p (l b t e) -> p l t b e", l=2, t=PACK, e=2),
+        )
+        nc.vector.tensor_copy(xb[:].rearrange("p (t b q) -> p b t q", t=PACK, q=8), word_tab[:].indirect(two_sb[:]))
+
+        def interleave(dst, src):
+            nc.scalar.copy(
+                dst.rearrange("p (c i j) -> p c j i", i=4, j=PACK), src.rearrange("p j (c i) -> p c j i", i=4)
+            )
+
+        def quantize(codes, scales, values):
+            nc.vector.quantize_mx(out=codes.bitcast(FP8X4), scales=scales, in_=values)
+
+        def matmul(acc, lhs, lhs_scales, rhs, rhs_scales):
+            nc.tensor.matmul_mx(
+                out=acc, lhsT=lhs.bitcast(FP8X4), lhsT_scale=lhs_scales, rhs=rhs.bitcast(FP8X4),
+                rhs_scale=rhs_scales, start=True, stop=True,
+            )
+
+        wa_codes = keep.tile([P, H], U32, name="wa_codes", align_bytes=64)
+        wa_scales = keep.tile([P, H], U8, name="wa_scales", align_bytes=64)
+        for h in range(2):
+            grouped = keep.tile([P, HALF * PACK], BF16, name=f"wa_grouped{h}", align_bytes=64)
+            interleave(grouped[:], wa_raw[h][:])
+            cols = slice(h * HALF, (h + 1) * HALF)
+            quantize(wa_codes[:, cols], wa_scales[:, cols], grouped[:])
+        a_sb = []
+        for t in range(PACK):
+            acc = psum.tile([P, H], F32, name=f"a_ps{t}", tag="acc", bufs=6)
+            cols = slice(t * P, (t + 1) * P)
+            matmul(acc[:], xa[:, cols], dealt_scales[:, cols], wa_codes[:], wa_scales[:])
+            a_t = keep.tile([P, H], F32, name=f"a{t}")
+            nc.scalar.copy(a_t[:], acc[:])
+            a_sb.append(a_t)
+
+        old = {}
+
+        def fetch_old(t, tag):
+            old[t] = keep.tile([P, N], F32, name=f"old{t}", tag=tag, align_bytes=64)
+            nc.vector.tensor_copy(old[t][:], page[t][:].indirect(n3_sb[:]))
+
+        fetch_old(0, "old0")
+
+        wb_grouped = keep.tile([P, N * PACK], BF16, name="wb_grouped", tag="dt1", align_bytes=64)
+        interleave(wb_grouped[:], wb_raw[:])
+        wb_codes = keep.tile([P, N], U32, name="wb_codes", align_bytes=64)
+        wb_scales = keep.tile([P, N], U8, name="wb_scales", align_bytes=64)
+        z2_rows = keep.tile([P, PACK, N], BF16, name="z2_rows")
+        z2_grouped = keep.tile([P, N * PACK], BF16, name="z2_grouped", align_bytes=64)
+        z2_codes = keep.tile([P, N], U32, name="z2_codes", align_bytes=64)
+        z2_scales = keep.tile([P, N], U8, name="z2_scales", align_bytes=64)
+
+        def project_b():
+            quantize(wb_codes[:], wb_scales[:], wb_grouped[:])
+            for t in range(PACK):
+                acc = psum.tile([P, N], F32, name=f"b_ps{t}", tag="acc", bufs=6)
+                matmul(acc[:], xb[:, t * P : (t + 1) * P], dealt_scales[:, S + t * P : S + (t + 1) * P],
+                       wb_codes[:], wb_scales[:])
+                nc.scalar.activation(z2_rows[:, t, :], acc[:], COPY, scale=gates[:, PACK + t : PACK + t + 1])
+            interleave(z2_grouped[:], z2_rows[:])
+
+        pa, pb, dt = {}, {}, {}
+        z_grouped = [keep.tile([P, 2, P, PACK], BF16, name=f"z_grouped{h}", tag=f"zg{h}", align_bytes=64) for h in range(2)]
+
+        def fetch_pa(t):
+            pa[t] = keep.tile([P, W], F32, name=f"pa{t}", tag=f"pa{t % 2}", align_bytes=64)
+            nc.vector.tensor_copy(pa[t][:], a_sb[t][:].indirect(n1_sb[:]))
+
+        def fetch_pb(t):
+            pb[t] = keep.tile([P, W], F32, name=f"pb{t}", tag=f"pb{t % 2}")
+            nc.vector.tensor_copy(pb[t][:], a_sb[t][:].indirect(n2_sb[:]))
+
+        def put_sum(t):
+            dt[t] = keep.tile([P, H], F32, name=f"dt{t}", tag=f"dt{t}", align_bytes=64)
+            nc.vector.tensor_tensor(dt[t][:].indirect(n1_sb[:]), pa[t][:], pb[t][:], ADD)
+
+        def put_product(t):
+            nc.vector.tensor_tensor(dt[t][:].indirect(n2_sb[:]), pa[t][:], pb[t][:], MULT)
+            cols = dt[t][:].rearrange("p (m u) -> p m u", u=PACK)
+            for h in range(2):
+                nc.scalar.activation(
+                    z_grouped[h][:, :, :, t].rearrange("p u m -> p m u"), cols[:, :, 2 * h : 2 * h + 2], COPY,
+                    scale=gates[:, t : t + 1],
+                )
+
+        fetch_pa(0)
+        fetch_pb(0)
+        for t in range(PACK - 1):
+            fetch_pa(t + 1)
+            put_sum(t)
+            fetch_pb(t + 1)
+            put_product(t)
+            if t == 0:
+                project_b()
+        put_sum(PACK - 1)
+        quantize(z2_codes[:], z2_scales[:], z2_grouped[:])
+        put_product(PACK - 1)
+
+        z_codes = keep.tile([P, H], U32, name="z_codes", align_bytes=64)
+        z_scales = keep.tile([P, H], U8, name="z_scales", align_bytes=64)
+        cv = []
+        fetch_old(1, "pa1")
+        for h in range(2):
+            cols = slice(h * HALF, (h + 1) * HALF)
+            quantize(z_codes[:, cols], z_scales[:, cols], z_grouped[h][:].rearrange("p u m t -> p (u m t)"))
+            fetch_old(2 + h, f"zg{h}")
+            for u in range(2 * h, 2 * h + 2):
+                acc = psum.tile([P, N], F32, name=f"cv_ps{u}", tag="acc", bufs=6)
+                matmul(acc[:], z_codes[:, u * P : (u + 1) * P], z_scales[:, u * P : (u + 1) * P],
+                       z2_codes[:], z2_scales[:])
+                cv_u = keep.tile([P, N], F32, name=f"cv{u}")
+                nc.scalar.activation(cv_u[:], acc[:], COPY, scale=0.0625)
+                cv.append(cv_u)
+        new = {}
+
+        def take_larger(u):
+            new[u] = keep.tile([P, N], F32, name=f"new{u}")
+            nc.vector.scalar_tensor_tensor(new[u][:], old[u][:], 0.5, cv[u][:], MULT, MAX)
+
+        take_larger(0)
+        for u in range(PACK):
+            if u + 1 < PACK:
+                take_larger(u + 1)
+            nc.vector.tensor_copy(page[u][:].indirect(n3_sb[:]), new[u][:])
+            nc.sync.dma_start(out_rows[u], page[u][:])

@@ -29,6 +29,7 @@ def tile_picked_mombondpagex_none_p_kernel(
     nc = tc.nc
     with ExitStack() as ctx:
         keep = ctx.enter_context(tc.tile_pool(name="keep", bufs=1))
+        reuse = ctx.enter_context(tc.tile_pool(name="reuse", bufs=1))
         psum = ctx.enter_context(tc.psum_pool(name="psum", bufs=1))
 
         def load_list(name, src):
@@ -37,7 +38,7 @@ def tile_picked_mombondpagex_none_p_kernel(
             return lst
 
         offs_sb = load_list("offs_sb", offs)
-        scale_tab = keep.tile([P, T], U8, name="scale_tab", align_bytes=64)
+        scale_tab = keep.tile([P, T], U8, name="scale_tab", tag="scale_tab", align_bytes=64)
         nc.gpsimd.memset(scale_tab[:].bitcast(I32), 0)
         for q in range(4):
             nc.scalar.dma_start(
@@ -45,55 +46,60 @@ def tile_picked_mombondpagex_none_p_kernel(
             )
         word_tab = keep.tile([P, T], U32, name="word_tab", align_bytes=64)
         words_in = x_words[0].rearrange("p n t -> p (n t)").bitcast(I32)
-        for h in range(2):
-            cols = slice(h * T // 2, (h + 1) * T // 2)
-            nc.sync.dma_start(word_tab[:].bitcast(I32)[:, cols], words_in[:, cols])
+        nc.sync.dma_start(word_tab[:].bitcast(I32), words_in)
         two_sb = load_list("two_sb", two)
 
         wa_rows = wa.rearrange("(p j) h -> p j h", j=PACK)
         wa_raw = []
         for h in range(2):
-            raw = keep.tile([P, PACK, HALF], F32, name=f"wa_raw{h}")
+            raw = keep.tile([P, PACK, HALF], F32, name=f"wa_raw{h}", tag=f"wa_raw{h}", align_bytes=64)
             nc.sync.dma_start(raw[:], wa_rows[:, :, h * HALF : (h + 1) * HALF])
             wa_raw.append(raw)
-        n1_sb = load_list("n1_sb", n1)
-        n2_sb = load_list("n2_sb", n2)
         n3_sb = load_list("n3_sb", n3)
         mem_rows = mem.rearrange("(p t) u -> t p u", t=PACK)
         out_rows = out.rearrange("(p t) u -> t p u", t=PACK)
         page = [keep.tile([P, U], F32, name=f"page{t}") for t in range(PACK)]
         nc.sync.dma_start(page[0][:], mem_rows[0])
-        wb_raw = keep.tile([P, PACK, N], F32, name="wb_raw")
+        n1_sb = load_list("n1_sb", n1)
+        n2_sb = load_list("n2_sb", n2)
+        wb_raw = reuse.tile([P, PACK, N], F32, name="wb_raw", offset=0)
         nc.sync.dma_start(wb_raw[:], wb.rearrange("(p j) n -> p j n", j=PACK))
-        for t in range(1, PACK):
-            nc.sync.dma_start(page[t][:], mem_rows[t])
-
         gate_rows = keep.tile([P, P], F32, name="gate_rows")
         ident = keep.tile([P, P], F32, name="ident")
         nc.gpsimd.memset(gate_rows[:], 0.0)
         make_identity(nc, ident[:])
         for g, src in enumerate((gt, gi)):
-            nc.scalar.dma_start(
+            nc.sync.dma_start(
                 gate_rows[PACK * g : PACK * (g + 1), :].rearrange("t (b q) -> t b q", q=8),
                 src.rearrange("(b t q) o -> t b (q o)", t=PACK, q=8),
             )
+        for t in range(1, PACK):
+            nc.sync.dma_start(page[t][:], mem_rows[t])
         gate_ps = psum.tile([P, P], F32, name="gate_ps")
         nc.tensor.transpose(gate_ps[:], gate_rows[:], ident[:])
         gates = keep.tile([P, 2 * PACK], F32, name="gates")
         nc.scalar.activation(gates[:], gate_ps[:, 0 : 2 * PACK], COPY)
 
-        picked_scales = keep.tile([P, 2 * S], U8, name="picked_scales", align_bytes=64)
-        nc.vector.tensor_copy(picked_scales[:, 0:S], scale_tab[:].indirect(offs_sb[:]))
-        nc.vector.tensor_copy(picked_scales[:, S : 2 * S], scale_tab[:].indirect(two_sb[:]))
-        xa = keep.tile([P, S], U32, name="xa", align_bytes=64)
-        xb = keep.tile([P, S], U32, name="xb", align_bytes=64)
-        nc.vector.tensor_copy(xa[:].rearrange("p (t b q) -> p b t q", t=PACK, q=8), word_tab[:].indirect(offs_sb[:]))
-        dealt_scales = keep.tile([P, 2 * S], U8, name="dealt_scales", align_bytes=64)
-        nc.vector.tensor_copy(
-            dealt_scales[:].bitcast(I32).rearrange("p (l t b e) -> p l t b e", l=2, t=PACK, e=2),
-            picked_scales[:].bitcast(I32).rearrange("p (l b t e) -> p l t b e", l=2, t=PACK, e=2),
-        )
-        nc.vector.tensor_copy(xb[:].rearrange("p (t b q) -> p b t q", t=PACK, q=8), word_tab[:].indirect(two_sb[:]))
+        def pick_words(name, lst):
+            words = keep.tile([P, S], U32, name=name, align_bytes=64)
+            nc.vector.tensor_copy(
+                words[:].rearrange("p (t b q) -> p b t q", t=PACK, q=8), word_tab[:].indirect(lst[:])
+            )
+            return words
+
+        def pick_scales(name, lst, tag):
+            picked = keep.tile([P, S], U8, name=f"{name}_picked", tag=tag, align_bytes=64)
+            nc.vector.tensor_copy(picked[:], scale_tab[:].indirect(lst[:]))
+            dealt = keep.tile([P, S], U8, name=name, align_bytes=64)
+            nc.vector.tensor_copy(
+                dealt[:].bitcast(I32).rearrange("p (t b e) -> p t b e", t=PACK, e=2),
+                picked[:].bitcast(I32).rearrange("p (b t e) -> p t b e", t=PACK, e=2),
+            )
+            return dealt
+
+        xa = pick_words("xa", offs_sb)
+        xa_scales = pick_scales("xa_scales", offs_sb, "xa_picked")
+        xb = pick_words("xb", two_sb)
 
         def interleave(dst, src):
             nc.scalar.copy(
@@ -112,106 +118,93 @@ def tile_picked_mombondpagex_none_p_kernel(
         wa_codes = keep.tile([P, H], U32, name="wa_codes", align_bytes=64)
         wa_scales = keep.tile([P, H], U8, name="wa_scales", align_bytes=64)
         for h in range(2):
-            grouped = keep.tile([P, HALF * PACK], BF16, name=f"wa_grouped{h}", align_bytes=64)
+            grouped = keep.tile([P, HALF * PACK], BF16, name=f"wa_grouped{h}", tag=f"wa_grouped{h}", align_bytes=64)
             interleave(grouped[:], wa_raw[h][:])
             cols = slice(h * HALF, (h + 1) * HALF)
             quantize(wa_codes[:, cols], wa_scales[:, cols], grouped[:])
         a_sb = []
         for t in range(PACK):
             acc = psum.tile([P, H], F32, name=f"a_ps{t}", tag="acc", bufs=6)
-            cols = slice(t * P, (t + 1) * P)
-            matmul(acc[:], xa[:, cols], dealt_scales[:, cols], wa_codes[:], wa_scales[:])
+            tok = slice(t * P, (t + 1) * P)
+            matmul(acc[:], xa[:, tok], xa_scales[:, tok], wa_codes[:], wa_scales[:])
             a_t = keep.tile([P, H], F32, name=f"a{t}")
             nc.scalar.copy(a_t[:], acc[:])
             a_sb.append(a_t)
+        xb_scales = pick_scales("xb_scales", two_sb, "wa_raw1")
 
-        old = {}
+        pa, pb = [], []
+        for t in range(PACK):
+            pa.append(keep.tile([P, W], F32, name=f"pa{t}", tag=f"pa{t}"))
+            pb.append(keep.tile([P, W], F32, name=f"pb{t}"))
+            nc.vector.tensor_copy(pa[t][:], a_sb[t][:].indirect(n1_sb[:]))
+            nc.vector.tensor_copy(pb[t][:], a_sb[t][:].indirect(n2_sb[:]))
 
-        def fetch_old(t, tag):
-            old[t] = keep.tile([P, N], F32, name=f"old{t}", tag=tag, align_bytes=64)
-            nc.vector.tensor_copy(old[t][:], page[t][:].indirect(n3_sb[:]))
-
-        fetch_old(0, "old0")
-
-        wb_grouped = keep.tile([P, N * PACK], BF16, name="wb_grouped", tag="dt1", align_bytes=64)
+        wb_grouped = keep.tile([P, N * PACK], BF16, name="wb_grouped", align_bytes=64)
         interleave(wb_grouped[:], wb_raw[:])
         wb_codes = keep.tile([P, N], U32, name="wb_codes", align_bytes=64)
         wb_scales = keep.tile([P, N], U8, name="wb_scales", align_bytes=64)
+        quantize(wb_codes[:], wb_scales[:], wb_grouped[:])
         z2_rows = keep.tile([P, PACK, N], BF16, name="z2_rows")
+        for t in range(PACK):
+            acc = psum.tile([P, N], F32, name=f"b_ps{t}", tag="acc", bufs=6)
+            tok = slice(t * P, (t + 1) * P)
+            matmul(acc[:], xb[:, tok], xb_scales[:, tok], wb_codes[:], wb_scales[:])
+            nc.scalar.activation(z2_rows[:, t, :], acc[:], COPY, scale=gates[:, PACK + t : PACK + t + 1])
         z2_grouped = keep.tile([P, N * PACK], BF16, name="z2_grouped", align_bytes=64)
-        z2_codes = keep.tile([P, N], U32, name="z2_codes", align_bytes=64)
-        z2_scales = keep.tile([P, N], U8, name="z2_scales", align_bytes=64)
+        interleave(z2_grouped[:], z2_rows[:])
 
-        def project_b():
-            quantize(wb_codes[:], wb_scales[:], wb_grouped[:])
-            for t in range(PACK):
-                acc = psum.tile([P, N], F32, name=f"b_ps{t}", tag="acc", bufs=6)
-                matmul(acc[:], xb[:, t * P : (t + 1) * P], dealt_scales[:, S + t * P : S + (t + 1) * P],
-                       wb_codes[:], wb_scales[:])
-                nc.scalar.activation(z2_rows[:, t, :], acc[:], COPY, scale=gates[:, PACK + t : PACK + t + 1])
-            interleave(z2_grouped[:], z2_rows[:])
-
-        pa, pb, dt = {}, {}, {}
-        z_grouped = [keep.tile([P, 2, P, PACK], BF16, name=f"z_grouped{h}", tag=f"zg{h}", align_bytes=64) for h in range(2)]
-
-        def fetch_pa(t):
-            pa[t] = keep.tile([P, W], F32, name=f"pa{t}", tag=f"pa{t % 2}", align_bytes=64)
-            nc.vector.tensor_copy(pa[t][:], a_sb[t][:].indirect(n1_sb[:]))
-
-        def fetch_pb(t):
-            pb[t] = keep.tile([P, W], F32, name=f"pb{t}", tag=f"pb{t % 2}")
-            nc.vector.tensor_copy(pb[t][:], a_sb[t][:].indirect(n2_sb[:]))
+        dt_place = (0, 1, 3, 2)
+        dt = [reuse.tile([P, H], F32, name=f"dt{t}", offset=dt_place[t] * H * 4) for t in range(PACK)]
+        z_grouped = [keep.tile([P, 2, P, PACK], BF16, name=f"z_grouped{h}", align_bytes=64) for h in range(2)]
 
         def put_sum(t):
-            dt[t] = keep.tile([P, H], F32, name=f"dt{t}", tag=f"dt{t}", align_bytes=64)
             nc.vector.tensor_tensor(dt[t][:].indirect(n1_sb[:]), pa[t][:], pb[t][:], ADD)
 
         def put_product(t):
             nc.vector.tensor_tensor(dt[t][:].indirect(n2_sb[:]), pa[t][:], pb[t][:], MULT)
+
+        def weigh(t, h):
             cols = dt[t][:].rearrange("p (m u) -> p m u", u=PACK)
-            for h in range(2):
-                nc.scalar.activation(
-                    z_grouped[h][:, :, :, t].rearrange("p u m -> p m u"), cols[:, :, 2 * h : 2 * h + 2], COPY,
-                    scale=gates[:, t : t + 1],
-                )
+            nc.scalar.activation(
+                z_grouped[h][:, :, :, t].rearrange("p u m -> p m u"), cols[:, :, 2 * h : 2 * h + 2], COPY,
+                scale=gates[:, t : t + 1],
+            )
 
-        fetch_pa(0)
-        fetch_pb(0)
-        for t in range(PACK - 1):
-            fetch_pa(t + 1)
-            put_sum(t)
-            fetch_pb(t + 1)
+        put_sum(0)
+        for t in range(PACK):
+            if t + 1 < PACK:
+                put_sum(t + 1)
             put_product(t)
-            if t == 0:
-                project_b()
-        put_sum(PACK - 1)
-        quantize(z2_codes[:], z2_scales[:], z2_grouped[:])
-        put_product(PACK - 1)
+        for t, h in ((0, 0), (0, 1), (1, 0), (1, 1), (2, 0), (3, 0), (2, 1), (3, 1)):
+            weigh(t, h)
 
+        old = [keep.tile([P, 2, N], F32, name="old0", tag="pa2"),
+               reuse.tile([P, 2, N], F32, name="old1", offset=dt_place[2] * H * 4)]
+
+        def fetch_old(h):
+            for e in range(2):
+                nc.vector.tensor_copy(old[h][:, e, :], page[2 * h + e][:].indirect(n3_sb[:]))
+
+        fetch_old(0)
+        z2_codes = keep.tile([P, N], U32, name="z2_codes", align_bytes=64)
+        z2_scales = keep.tile([P, N], U8, name="z2_scales", align_bytes=64)
+        quantize(z2_codes[:], z2_scales[:], z2_grouped[:])
         z_codes = keep.tile([P, H], U32, name="z_codes", align_bytes=64)
         z_scales = keep.tile([P, H], U8, name="z_scales", align_bytes=64)
-        cv = []
-        fetch_old(1, "pa1")
+        cv = [keep.tile([P, 2, N], F32, name=f"cv{h}") for h in range(2)]
         for h in range(2):
             cols = slice(h * HALF, (h + 1) * HALF)
             quantize(z_codes[:, cols], z_scales[:, cols], z_grouped[h][:].rearrange("p u m t -> p (u m t)"))
-            fetch_old(2 + h, f"zg{h}")
-            for u in range(2 * h, 2 * h + 2):
-                acc = psum.tile([P, N], F32, name=f"cv_ps{u}", tag="acc", bufs=6)
-                matmul(acc[:], z_codes[:, u * P : (u + 1) * P], z_scales[:, u * P : (u + 1) * P],
-                       z2_codes[:], z2_scales[:])
-                cv_u = keep.tile([P, N], F32, name=f"cv{u}")
-                nc.scalar.activation(cv_u[:], acc[:], COPY, scale=0.0625)
-                cv.append(cv_u)
-        new = {}
-
-        def take_larger(u):
-            new[u] = keep.tile([P, N], F32, name=f"new{u}")
-            nc.vector.scalar_tensor_tensor(new[u][:], old[u][:], 0.5, cv[u][:], MULT, MAX)
-
-        take_larger(0)
-        for u in range(PACK):
-            if u + 1 < PACK:
-                take_larger(u + 1)
-            nc.vector.tensor_copy(page[u][:].indirect(n3_sb[:]), new[u][:])
-            nc.sync.dma_start(out_rows[u], page[u][:])
+            for e in range(2):
+                acc = psum.tile([P, N], F32, name=f"cv_ps{h}{e}", tag="acc", bufs=6)
+                rows = slice((2 * h + e) * P, (2 * h + e + 1) * P)
+                matmul(acc[:], z_codes[:, rows], z_scales[:, rows], z2_codes[:], z2_scales[:])
+                nc.scalar.activation(cv[h][:, e, :], acc[:], COPY, scale=0.0625)
+        fetch_old(1)
+        for h in range(2):
+            new = keep.tile([P, 2, N], F32, name=f"new{h}")
+            nc.vector.scalar_tensor_tensor(new[:], old[h][:], 0.5, cv[h][:], MULT, MAX)
+            for e in range(2):
+                u = 2 * h + e
+                nc.vector.tensor_copy(page[u][:].indirect(n3_sb[:]), new[:, e, :])
+                nc.sync.dma_start(out_rows[u], page[u][:])

@@ -103,7 +103,7 @@ def tile_picked_mombondpagex_none_p_kernel(
 
         def interleave(dst, src):
             nc.scalar.copy(
-                dst.rearrange("p (c i j) -> p c j i", i=4, j=PACK), src.rearrange("p j (c i) -> p c j i", i=4)
+                dst.rearrange("p (c i j) -> p c j i", i=2, j=PACK), src.rearrange("p j (c i) -> p c j i", i=2)
             )
 
         def quantize(codes, scales, values):
@@ -153,8 +153,10 @@ def tile_picked_mombondpagex_none_p_kernel(
         z2_grouped = keep.tile([P, N * PACK], BF16, name="z2_grouped", align_bytes=64)
         interleave(z2_grouped[:], z2_rows[:])
 
-        dt_place = (0, 1, 3, 2)
-        dt = [reuse.tile([P, H], F32, name=f"dt{t}", offset=dt_place[t] * H * 4) for t in range(PACK)]
+        dt_place = {1: 0, 3: 1, 2: 2}
+        dt = [keep.tile([P, H], F32, name="dt0")]
+        for t in range(1, PACK):
+            dt.append(reuse.tile([P, H], F32, name=f"dt{t}", offset=dt_place[t] * H * 4))
         z_grouped = [keep.tile([P, 2, P, PACK], BF16, name=f"z_grouped{h}", align_bytes=64) for h in range(2)]
 
         def put_sum(t):

@@ -38,23 +38,20 @@ def tile_picked_mombondpagex_none_p_kernel(
             return lst
 
         offs_sb = load_list("offs_sb", offs)
-        scale_tab = keep.tile([P, T], U8, name="scale_tab", tag="scale_tab", align_bytes=64)
+        scale_tab = keep.tile([P, T], U8, name="scale_tab", align_bytes=64)
         nc.gpsimd.memset(scale_tab[:].bitcast(I32), 0)
         for q in range(4):
-            nc.scalar.dma_start(
+            queue = nc.sync if q % 2 else nc.scalar
+            queue.dma_start(
                 scale_tab[32 * q : 32 * q + 4, :].bitcast(I32), x_scales[0, 4 * q : 4 * q + 4, :].bitcast(I32)
             )
-        word_tab = keep.tile([P, T], U32, name="word_tab", align_bytes=64)
-        words_in = x_words[0].rearrange("p n t -> p (n t)").bitcast(I32)
-        nc.sync.dma_start(word_tab[:].bitcast(I32), words_in)
-        two_sb = load_list("two_sb", two)
-
         wa_rows = wa.rearrange("(p j) h -> p j h", j=PACK)
-        wa_raw = []
-        for h in range(2):
-            raw = keep.tile([P, PACK, HALF], F32, name=f"wa_raw{h}", tag=f"wa_raw{h}", align_bytes=64)
-            nc.sync.dma_start(raw[:], wa_rows[:, :, h * HALF : (h + 1) * HALF])
-            wa_raw.append(raw)
+        wa_raw = [keep.tile([P, PACK, HALF], F32, name=f"wa_raw{h}") for h in range(2)]
+        nc.sync.dma_start(wa_raw[0][:], wa_rows[:, :, 0:HALF])
+        two_sb = load_list("two_sb", two)
+        nc.sync.dma_start(wa_raw[1][:], wa_rows[:, :, HALF:H])
+        word_tab = keep.tile([P, T], U32, name="word_tab", align_bytes=64)
+        nc.sync.dma_start(word_tab[:].bitcast(I32), x_words[0].rearrange("p n t -> p (n t)").bitcast(I32))
         n3_sb = load_list("n3_sb", n3)
         mem_rows = mem.rearrange("(p t) u -> t p u", t=PACK)
         out_rows = out.rearrange("(p t) u -> t p u", t=PACK)
@@ -97,8 +94,9 @@ def tile_picked_mombondpagex_none_p_kernel(
             )
             return dealt
 
-        xa = pick_words("xa", offs_sb)
         xa_scales = pick_scales("xa_scales", offs_sb, "xa_picked")
+        xb_scales = pick_scales("xb_scales", two_sb, "xb_picked")
+        xa = pick_words("xa", offs_sb)
         xb = pick_words("xb", two_sb)
 
         def interleave(dst, src):
@@ -130,7 +128,12 @@ def tile_picked_mombondpagex_none_p_kernel(
             a_t = keep.tile([P, H], F32, name=f"a{t}")
             nc.scalar.copy(a_t[:], acc[:])
             a_sb.append(a_t)
-        xb_scales = pick_scales("xb_scales", two_sb, "wa_raw1")
+
+        def fetch_old(u, dst):
+            nc.vector.tensor_copy(dst, page[u][:].indirect(n3_sb[:]))
+
+        old0 = keep.tile([P, N], F32, name="old0")
+        fetch_old(0, old0[:])
 
         pa, pb = [], []
         for t in range(PACK):
@@ -180,14 +183,8 @@ def tile_picked_mombondpagex_none_p_kernel(
         for t, h in ((0, 0), (0, 1), (1, 0), (1, 1), (2, 0), (3, 0), (2, 1), (3, 1)):
             weigh(t, h)
 
-        old = [keep.tile([P, 2, N], F32, name="old0", tag="pa2"),
-               reuse.tile([P, 2, N], F32, name="old1", offset=dt_place[2] * H * 4)]
-
-        def fetch_old(h):
-            for e in range(2):
-                nc.vector.tensor_copy(old[h][:, e, :], page[2 * h + e][:].indirect(n3_sb[:]))
-
-        fetch_old(0)
+        old1 = keep.tile([P, N], F32, name="old1", tag="pa2")
+        fetch_old(1, old1[:])
         z2_codes = keep.tile([P, N], U32, name="z2_codes", align_bytes=64)
         z2_scales = keep.tile([P, N], U8, name="z2_scales", align_bytes=64)
         quantize(z2_codes[:], z2_scales[:], z2_grouped[:])
@@ -202,11 +199,13 @@ def tile_picked_mombondpagex_none_p_kernel(
                 rows = slice((2 * h + e) * P, (2 * h + e + 1) * P)
                 matmul(acc[:], z_codes[:, rows], z_scales[:, rows], z2_codes[:], z2_scales[:])
                 nc.scalar.activation(cv[h][:, e, :], acc[:], COPY, scale=0.0625)
-        fetch_old(1)
-        for h in range(2):
-            new = keep.tile([P, 2, N], F32, name=f"new{h}")
-            nc.vector.scalar_tensor_tensor(new[:], old[h][:], 0.5, cv[h][:], MULT, MAX)
-            for e in range(2):
-                u = 2 * h + e
-                nc.vector.tensor_copy(page[u][:].indirect(n3_sb[:]), new[:, e, :])
-                nc.sync.dma_start(out_rows[u], page[u][:])
+        old23 = reuse.tile([P, 2, N], F32, name="old23", offset=dt_place[2] * H * 4)
+        for e in range(2):
+            fetch_old(2 + e, old23[:, e, :])
+        new = keep.tile([P, PACK, N], F32, name="new")
+        nc.vector.scalar_tensor_tensor(new[:, 0, :], old0[:], 0.5, cv[0][:, 0, :], MULT, MAX)
+        nc.vector.scalar_tensor_tensor(new[:, 1, :], old1[:], 0.5, cv[0][:, 1, :], MULT, MAX)
+        nc.vector.scalar_tensor_tensor(new[:, 2:4, :], old23[:], 0.5, cv[1][:], MULT, MAX)
+        for u in range(PACK):
+            nc.vector.tensor_copy(page[u][:].indirect(n3_sb[:]), new[:, u, :])
+            nc.sync.dma_start(out_rows[u], page[u][:])

@@ -20,7 +20,11 @@ MAX = mybir.AluOpType.max
 
 P = 128
 PACK = 4
+RUN = 8
+QUADRANT = 32
 HALF = H // 2
+ALIGN = 64
+PRODUCT_BANKS = 6
 
 
 def tile_picked_mombondpagex_none_p_kernel(
@@ -38,64 +42,66 @@ def tile_picked_mombondpagex_none_p_kernel(
             return lst
 
         offs_sb = load_list("offs_sb", offs)
-        scale_tab = keep.tile([P, T], U8, name="scale_tab", align_bytes=64)
+        scale_tab = keep.tile([P, T], U8, name="scale_tab", align_bytes=ALIGN)
         nc.gpsimd.memset(scale_tab[:].bitcast(I32), 0)
-        for q in range(4):
-            queue = nc.sync if q % 2 else nc.scalar
+        for quad in range(P // QUADRANT):
+            queue = nc.sync if quad % 2 else nc.scalar
             queue.dma_start(
-                scale_tab[32 * q : 32 * q + 4, :].bitcast(I32), x_scales[0, 4 * q : 4 * q + 4, :].bitcast(I32)
+                scale_tab[QUADRANT * quad : QUADRANT * quad + PACK, :].bitcast(I32),
+                x_scales[0, PACK * quad : PACK * (quad + 1), :].bitcast(I32),
             )
         wa_rows = wa.rearrange("(p j) h -> p j h", j=PACK)
-        wa_raw = [keep.tile([P, PACK, HALF], F32, name=f"wa_raw{h}") for h in range(2)]
+        wa_raw = [keep.tile([P, PACK, HALF], F32, name=f"wa_raw{half}") for half in range(2)]
         nc.sync.dma_start(wa_raw[0][:], wa_rows[:, :, 0:HALF])
         two_sb = load_list("two_sb", two)
         nc.sync.dma_start(wa_raw[1][:], wa_rows[:, :, HALF:H])
-        word_tab = keep.tile([P, T], U32, name="word_tab", align_bytes=64)
-        nc.sync.dma_start(word_tab[:].bitcast(I32), x_words[0].rearrange("p n t -> p (n t)").bitcast(I32))
+        word_tab = keep.tile([P, T], U32, name="word_tab", align_bytes=ALIGN)
+        nc.sync.dma_start(word_tab[:].bitcast(I32), x_words[0].rearrange("p n j -> p (n j)").bitcast(I32))
         n3_sb = load_list("n3_sb", n3)
-        mem_rows = mem.rearrange("(p t) u -> t p u", t=PACK)
-        out_rows = out.rearrange("(p t) u -> t p u", t=PACK)
-        page = [keep.tile([P, U], F32, name=f"page{t}") for t in range(PACK)]
+        mem_rows = mem.rearrange("(p u) w -> u p w", u=PACK)
+        out_rows = out.rearrange("(p u) w -> u p w", u=PACK)
+        page = [keep.tile([P, U], F32, name=f"page{u}") for u in range(PACK)]
         nc.sync.dma_start(page[0][:], mem_rows[0])
         n1_sb = load_list("n1_sb", n1)
         n2_sb = load_list("n2_sb", n2)
         wb_raw = reuse.tile([P, PACK, N], F32, name="wb_raw", offset=0)
         nc.sync.dma_start(wb_raw[:], wb.rearrange("(p j) n -> p j n", j=PACK))
+
         gate_rows = keep.tile([P, P], F32, name="gate_rows")
         ident = keep.tile([P, P], F32, name="ident")
         nc.gpsimd.memset(gate_rows[:], 0.0)
         make_identity(nc, ident[:])
-        for g, src in enumerate((gt, gi)):
+        for which, src in enumerate((gt, gi)):
             nc.sync.dma_start(
-                gate_rows[PACK * g : PACK * (g + 1), :].rearrange("t (b q) -> t b q", q=8),
-                src.rearrange("(b t q) o -> t b (q o)", t=PACK, q=8),
+                gate_rows[PACK * which : PACK * (which + 1), :].rearrange("t (g q) -> t g q", q=RUN),
+                src.rearrange("(g t q) o -> t g (q o)", t=PACK, q=RUN),
             )
-        for t in range(1, PACK):
-            nc.sync.dma_start(page[t][:], mem_rows[t])
+        for u in range(1, PACK):
+            nc.sync.dma_start(page[u][:], mem_rows[u])
         gate_ps = psum.tile([P, P], F32, name="gate_ps")
         nc.tensor.transpose(gate_ps[:], gate_rows[:], ident[:])
         gates = keep.tile([P, 2 * PACK], F32, name="gates")
         nc.scalar.activation(gates[:], gate_ps[:, 0 : 2 * PACK], COPY)
 
         def pick_words(name, lst):
-            words = keep.tile([P, S], U32, name=name, align_bytes=64)
+            words = keep.tile([P, S], U32, name=name, align_bytes=ALIGN)
             nc.vector.tensor_copy(
-                words[:].rearrange("p (t b q) -> p b t q", t=PACK, q=8), word_tab[:].indirect(lst[:])
+                words[:].rearrange("p (t g q) -> p g t q", t=PACK, q=RUN), word_tab[:].indirect(lst[:])
             )
             return words
 
-        def pick_scales(name, lst, tag):
-            picked = keep.tile([P, S], U8, name=f"{name}_picked", tag=tag, align_bytes=64)
+        def pick_scales(name, lst):
+            picked = keep.tile([P, S], U8, name=f"{name}_picked", align_bytes=ALIGN)
             nc.vector.tensor_copy(picked[:], scale_tab[:].indirect(lst[:]))
-            dealt = keep.tile([P, S], U8, name=name, align_bytes=64)
+            dealt = keep.tile([P, S], U8, name=name, align_bytes=ALIGN)
             nc.vector.tensor_copy(
-                dealt[:].bitcast(I32).rearrange("p (t b e) -> p t b e", t=PACK, e=2),
-                picked[:].bitcast(I32).rearrange("p (b t e) -> p t b e", t=PACK, e=2),
+                dealt[:].bitcast(I32).rearrange("p (t g w) -> p t g w", t=PACK, w=2),
+                picked[:].bitcast(I32).rearrange("p (g t w) -> p t g w", t=PACK, w=2),
             )
             return dealt
 
-        xa_scales = pick_scales("xa_scales", offs_sb, "xa_picked")
-        xb_scales = pick_scales("xb_scales", two_sb, "xb_picked")
+        xa_scales = pick_scales("xa_scales", offs_sb)
+        xb_scales = pick_scales("xb_scales", two_sb)
         xa = pick_words("xa", offs_sb)
         xb = pick_words("xb", two_sb)
 
@@ -107,27 +113,32 @@ def tile_picked_mombondpagex_none_p_kernel(
         def quantize(codes, scales, values):
             nc.vector.quantize_mx(out=codes.bitcast(FP8X4), scales=scales, in_=values)
 
-        def matmul(acc, lhs, lhs_scales, rhs, rhs_scales):
+        def product(name, lhs, lhs_scales, rhs, rhs_scales):
+            acc = psum.tile([P, rhs.shape[1]], F32, name=name, tag="product", bufs=PRODUCT_BANKS)
             nc.tensor.matmul_mx(
-                out=acc, lhsT=lhs.bitcast(FP8X4), lhsT_scale=lhs_scales, rhs=rhs.bitcast(FP8X4),
-                rhs_scale=rhs_scales, start=True, stop=True,
+                out=acc[:],
+                lhsT=lhs.bitcast(FP8X4),
+                lhsT_scale=lhs_scales,
+                rhs=rhs.bitcast(FP8X4),
+                rhs_scale=rhs_scales,
+                start=True,
+                stop=True,
             )
+            return acc
 
-        wa_codes = keep.tile([P, H], U32, name="wa_codes", align_bytes=64)
-        wa_scales = keep.tile([P, H], U8, name="wa_scales", align_bytes=64)
-        for h in range(2):
-            grouped = keep.tile([P, HALF * PACK], BF16, name=f"wa_grouped{h}", tag=f"wa_grouped{h}", align_bytes=64)
-            interleave(grouped[:], wa_raw[h][:])
-            cols = slice(h * HALF, (h + 1) * HALF)
-            quantize(wa_codes[:, cols], wa_scales[:, cols], grouped[:])
-        a_sb = []
+        wa_codes = keep.tile([P, H], U32, name="wa_codes", align_bytes=ALIGN)
+        wa_scales = keep.tile([P, H], U8, name="wa_scales", align_bytes=ALIGN)
+        for half in range(2):
+            wa_grouped = keep.tile([P, HALF * PACK], BF16, name=f"wa_grouped{half}", align_bytes=ALIGN)
+            interleave(wa_grouped[:], wa_raw[half][:])
+            cols = slice(half * HALF, (half + 1) * HALF)
+            quantize(wa_codes[:, cols], wa_scales[:, cols], wa_grouped[:])
+        a = []
         for t in range(PACK):
-            acc = psum.tile([P, H], F32, name=f"a_ps{t}", tag="acc", bufs=6)
-            tok = slice(t * P, (t + 1) * P)
-            matmul(acc[:], xa[:, tok], xa_scales[:, tok], wa_codes[:], wa_scales[:])
-            a_t = keep.tile([P, H], F32, name=f"a{t}")
-            nc.scalar.copy(a_t[:], acc[:])
-            a_sb.append(a_t)
+            tokens = slice(t * P, (t + 1) * P)
+            acc = product(f"a_ps{t}", xa[:, tokens], xa_scales[:, tokens], wa_codes[:], wa_scales[:])
+            a.append(keep.tile([P, H], F32, name=f"a{t}"))
+            nc.scalar.copy(a[t][:], acc[:])
 
         def fetch_old(u, dst):
             nc.vector.tensor_copy(dst, page[u][:].indirect(n3_sb[:]))
@@ -137,30 +148,31 @@ def tile_picked_mombondpagex_none_p_kernel(
 
         pa, pb = [], []
         for t in range(PACK):
-            pa.append(keep.tile([P, W], F32, name=f"pa{t}", tag=f"pa{t}"))
+            pa.append(keep.tile([P, W], F32, name=f"pa{t}"))
             pb.append(keep.tile([P, W], F32, name=f"pb{t}"))
-            nc.vector.tensor_copy(pa[t][:], a_sb[t][:].indirect(n1_sb[:]))
-            nc.vector.tensor_copy(pb[t][:], a_sb[t][:].indirect(n2_sb[:]))
+            nc.vector.tensor_copy(pa[t][:], a[t][:].indirect(n1_sb[:]))
+            nc.vector.tensor_copy(pb[t][:], a[t][:].indirect(n2_sb[:]))
 
-        wb_grouped = keep.tile([P, N * PACK], BF16, name="wb_grouped", align_bytes=64)
+        wb_grouped = keep.tile([P, N * PACK], BF16, name="wb_grouped", align_bytes=ALIGN)
         interleave(wb_grouped[:], wb_raw[:])
-        wb_codes = keep.tile([P, N], U32, name="wb_codes", align_bytes=64)
-        wb_scales = keep.tile([P, N], U8, name="wb_scales", align_bytes=64)
+        wb_codes = keep.tile([P, N], U32, name="wb_codes", align_bytes=ALIGN)
+        wb_scales = keep.tile([P, N], U8, name="wb_scales", align_bytes=ALIGN)
         quantize(wb_codes[:], wb_scales[:], wb_grouped[:])
         z2_rows = keep.tile([P, PACK, N], BF16, name="z2_rows")
         for t in range(PACK):
-            acc = psum.tile([P, N], F32, name=f"b_ps{t}", tag="acc", bufs=6)
-            tok = slice(t * P, (t + 1) * P)
-            matmul(acc[:], xb[:, tok], xb_scales[:, tok], wb_codes[:], wb_scales[:])
+            tokens = slice(t * P, (t + 1) * P)
+            acc = product(f"b_ps{t}", xb[:, tokens], xb_scales[:, tokens], wb_codes[:], wb_scales[:])
             nc.scalar.activation(z2_rows[:, t, :], acc[:], COPY, scale=gates[:, PACK + t : PACK + t + 1])
-        z2_grouped = keep.tile([P, N * PACK], BF16, name="z2_grouped", align_bytes=64)
+        z2_grouped = keep.tile([P, N * PACK], BF16, name="z2_grouped", align_bytes=ALIGN)
         interleave(z2_grouped[:], z2_rows[:])
 
-        dt_place = {1: 0, 3: 1, 2: 2}
         dt = [keep.tile([P, H], F32, name="dt0")]
         for t in range(1, PACK):
-            dt.append(reuse.tile([P, H], F32, name=f"dt{t}", offset=dt_place[t] * H * 4))
-        z_grouped = [keep.tile([P, 2, P, PACK], BF16, name=f"z_grouped{h}", align_bytes=64) for h in range(2)]
+            dt.append(reuse.tile([P, H], F32, name=f"dt{t}", offset=(t - 1) * H * 4))
+        z_rows = [keep.tile([P, PACK, P, 2], BF16, name=f"z_rows{half}") for half in range(2)]
+        z_grouped = [
+            keep.tile([P, 2, P, PACK], BF16, name=f"z_grouped{half}", align_bytes=ALIGN) for half in range(2)
+        ]
 
         def put_sum(t):
             nc.vector.tensor_tensor(dt[t][:].indirect(n1_sb[:]), pa[t][:], pb[t][:], ADD)
@@ -168,44 +180,44 @@ def tile_picked_mombondpagex_none_p_kernel(
         def put_product(t):
             nc.vector.tensor_tensor(dt[t][:].indirect(n2_sb[:]), pa[t][:], pb[t][:], MULT)
 
-        def weigh(t, h):
-            cols = dt[t][:].rearrange("p (m u) -> p m u", u=PACK)
-            nc.scalar.activation(
-                z_grouped[h][:, :, :, t].rearrange("p u m -> p m u"), cols[:, :, 2 * h : 2 * h + 2], COPY,
-                scale=gates[:, t : t + 1],
-            )
+        def weigh(t, half):
+            cols = dt[t][:].rearrange("p (m u) -> p m u", u=PACK)[:, :, 2 * half : 2 * half + 2]
+            nc.scalar.activation(z_rows[half][:, t], cols, COPY, scale=gates[:, t : t + 1])
 
         put_sum(0)
         for t in range(PACK):
             if t + 1 < PACK:
                 put_sum(t + 1)
             put_product(t)
-        for t, h in ((0, 0), (0, 1), (1, 0), (1, 1), (2, 0), (3, 0), (2, 1), (3, 1)):
-            weigh(t, h)
+        for t in range(PACK - 1):
+            for half in range(2):
+                weigh(t, half)
+        for half in range(2):
+            weigh(PACK - 1, half)
+            nc.scalar.copy(z_grouped[half][:], z_rows[half][:].rearrange("p t m e -> p e m t"))
 
-        old1 = keep.tile([P, N], F32, name="old1", tag="pa2")
-        fetch_old(1, old1[:])
-        z2_codes = keep.tile([P, N], U32, name="z2_codes", align_bytes=64)
-        z2_scales = keep.tile([P, N], U8, name="z2_scales", align_bytes=64)
-        quantize(z2_codes[:], z2_scales[:], z2_grouped[:])
-        z_codes = keep.tile([P, H], U32, name="z_codes", align_bytes=64)
-        z_scales = keep.tile([P, H], U8, name="z_scales", align_bytes=64)
-        cv = [keep.tile([P, 2, N], F32, name=f"cv{h}") for h in range(2)]
-        for h in range(2):
-            cols = slice(h * HALF, (h + 1) * HALF)
-            quantize(z_codes[:, cols], z_scales[:, cols], z_grouped[h][:].rearrange("p u m t -> p (u m t)"))
-            for e in range(2):
-                acc = psum.tile([P, N], F32, name=f"cv_ps{h}{e}", tag="acc", bufs=6)
-                rows = slice((2 * h + e) * P, (2 * h + e + 1) * P)
-                matmul(acc[:], z_codes[:, rows], z_scales[:, rows], z2_codes[:], z2_scales[:])
-                nc.scalar.activation(cv[h][:, e, :], acc[:], COPY, scale=0.0625)
-        old23 = reuse.tile([P, 2, N], F32, name="old23", offset=dt_place[2] * H * 4)
+        old12 = keep.tile([P, 2, N], F32, name="old12", tag="pa2")
         for e in range(2):
-            fetch_old(2 + e, old23[:, e, :])
-        new = keep.tile([P, PACK, N], F32, name="new")
-        nc.vector.scalar_tensor_tensor(new[:, 0, :], old0[:], 0.5, cv[0][:, 0, :], MULT, MAX)
-        nc.vector.scalar_tensor_tensor(new[:, 1, :], old1[:], 0.5, cv[0][:, 1, :], MULT, MAX)
-        nc.vector.scalar_tensor_tensor(new[:, 2:4, :], old23[:], 0.5, cv[1][:], MULT, MAX)
+            fetch_old(1 + e, old12[:, e, :])
+        z2_codes = keep.tile([P, N], U32, name="z2_codes", align_bytes=ALIGN)
+        z2_scales = keep.tile([P, N], U8, name="z2_scales", align_bytes=ALIGN)
+        quantize(z2_codes[:], z2_scales[:], z2_grouped[:])
+        z_codes = keep.tile([P, H], U32, name="z_codes", align_bytes=ALIGN)
+        z_scales = keep.tile([P, H], U8, name="z_scales", align_bytes=ALIGN)
+        cv = keep.tile([P, PACK, N], F32, name="cv")
+        for half in range(2):
+            cols = slice(half * HALF, (half + 1) * HALF)
+            quantize(z_codes[:, cols], z_scales[:, cols], z_grouped[half][:].rearrange("p e m t -> p (e m t)"))
+            for u in range(2 * half, 2 * half + 2):
+                rows = slice(u * P, (u + 1) * P)
+                acc = product(f"cv_ps{u}", z_codes[:, rows], z_scales[:, rows], z2_codes[:], z2_scales[:])
+                nc.scalar.activation(cv[:, u, :], acc[:], COPY, scale=0.0625)
+        old3 = keep.tile([P, N], F32, name="old3", tag="z_rows0")
+        fetch_old(3, old3[:])
+        nw = keep.tile([P, PACK, N], F32, name="nw")
+        nc.vector.scalar_tensor_tensor(nw[:, 0, :], old0[:], 0.5, cv[:, 0, :], MULT, MAX)
+        nc.vector.scalar_tensor_tensor(nw[:, 1:3, :], old12[:], 0.5, cv[:, 1:3, :], MULT, MAX)
+        nc.vector.scalar_tensor_tensor(nw[:, 3, :], old3[:], 0.5, cv[:, 3, :], MULT, MAX)
         for u in range(PACK):
-            nc.vector.tensor_copy(page[u][:].indirect(n3_sb[:]), new[:, u, :])
+            nc.vector.tensor_copy(page[u][:].indirect(n3_sb[:]), nw[:, u, :])
             nc.sync.dma_start(out_rows[u], page[u][:])

from contextlib import ExitStack

import concourse.mybir as mybir
from concourse.masks import make_identity

K, T, S, N, H, W, U = 512, 2048, 512, 512, 512, 256, 1024
FLOPS = 2 * K * S * H + 2 * K * S * N + 2 * S * H * N

F32 = mybir.dt.float32
BF16 = mybir.dt.bfloat16
I32 = mybir.dt.int32
U32 = mybir.dt.uint32
U16 = mybir.dt.uint16
U8 = mybir.dt.uint8
FP8X4 = mybir.dt.float8_e4m3fn_x4
COPY = mybir.ActivationFunctionType.Copy
ADD = mybir.AluOpType.add
MULT = mybir.AluOpType.mult
MAX = mybir.AluOpType.max

P = 128
PACK = 4
RUN = 8
QUADRANT = 32
HALF = H // 2
ALIGN = 64
PRODUCT_BANKS = 6


def tile_picked_mombondpagex_none_p_kernel(
    tc, x_words, x_scales, wa, wb, gt, gi, mem, offs, two, n1, n2, n3, out
):
    nc = tc.nc
    with ExitStack() as ctx:
        keep = ctx.enter_context(tc.tile_pool(name="keep", bufs=1))
        reuse = ctx.enter_context(tc.tile_pool(name="reuse", bufs=1))
        psum = ctx.enter_context(tc.psum_pool(name="psum", bufs=1))

        def load_list(name, src):
            lst = keep.tile(list(src.shape), U16, name=name)
            nc.sync.dma_start(lst[:], src)
            return lst

        offs_sb = load_list("offs_sb", offs)
        scale_tab = keep.tile([P, T], U8, name="scale_tab", align_bytes=ALIGN)
        nc.gpsimd.memset(scale_tab[:].bitcast(I32), 0)
        for quad in range(P // QUADRANT):
            queue = nc.sync if quad % 2 else nc.scalar
            queue.dma_start(
                scale_tab[QUADRANT * quad : QUADRANT * quad + PACK, :].bitcast(I32),
                x_scales[0, PACK * quad : PACK * (quad + 1), :].bitcast(I32),
            )
        wa_rows = wa.rearrange("(p j) h -> p j h", j=PACK)
        wa_raw = [keep.tile([P, PACK, HALF], F32, name=f"wa_raw{half}") for half in range(2)]
        nc.sync.dma_start(wa_raw[0][:], wa_rows[:, :, 0:HALF])
        two_sb = load_list("two_sb", two)
        nc.sync.dma_start(wa_raw[1][:], wa_rows[:, :, HALF:H])
        word_tab = keep.tile([P, T], U32, name="word_tab", align_bytes=ALIGN)
        nc.sync.dma_start(word_tab[:].bitcast(I32), x_words[0].rearrange("p n j -> p (n j)").bitcast(I32))
        n3_sb = load_list("n3_sb", n3)
        mem_rows = mem.rearrange("(p u) w -> u p w", u=PACK)
        out_rows = out.rearrange("(p u) w -> u p w", u=PACK)
        page = [keep.tile([P, U], F32, name=f"page{u}") for u in range(PACK)]
        nc.sync.dma_start(page[0][:], mem_rows[0])
        n1_sb = load_list("n1_sb", n1)
        n2_sb = load_list("n2_sb", n2)
        wb_raw = reuse.tile([P, PACK, N], F32, name="wb_raw", offset=0)
        nc.sync.dma_start(wb_raw[:], wb.rearrange("(p j) n -> p j n", j=PACK))

        gate_rows = keep.tile([P, P], F32, name="gate_rows")
        ident = keep.tile([P, P], F32, name="ident")
        nc.gpsimd.memset(gate_rows[:], 0.0)
        make_identity(nc, ident[:])
        for which, src in enumerate((gt, gi)):
            nc.sync.dma_start(
                gate_rows[PACK * which : PACK * (which + 1), :].rearrange("t (g q) -> t g q", q=RUN),
                src.rearrange("(g t q) o -> t g (q o)", t=PACK, q=RUN),
            )
        for u in range(1, PACK):
            nc.sync.dma_start(page[u][:], mem_rows[u])
        gate_ps = psum.tile([P, P], F32, name="gate_ps")
        nc.tensor.transpose(gate_ps[:], gate_rows[:], ident[:])
        gates = keep.tile([P, 2 * PACK], F32, name="gates")
        nc.scalar.activation(gates[:], gate_ps[:, 0 : 2 * PACK], COPY)

        def pick_words(name, lst):
            words = keep.tile([P, S], U32, name=name, align_bytes=ALIGN)
            nc.vector.tensor_copy(
                words[:].rearrange("p (t g q) -> p g t q", t=PACK, q=RUN), word_tab[:].indirect(lst[:])
            )
            return words

        def pick_scales(name, lst):
            picked = keep.tile([P, S], U8, name=f"{name}_picked", align_bytes=ALIGN)
            nc.vector.tensor_copy(picked[:], scale_tab[:].indirect(lst[:]))
            dealt = keep.tile([P, S], U8, name=name, align_bytes=ALIGN)
            nc.vector.tensor_copy(
                dealt[:].bitcast(I32).rearrange("p (t g w) -> p t g w", t=PACK, w=2),
                picked[:].bitcast(I32).rearrange("p (g t w) -> p t g w", t=PACK, w=2),
            )
            return dealt

        xa_scales = pick_scales("xa_scales", offs_sb)
        xb_scales = pick_scales("xb_scales", two_sb)
        xa = pick_words("xa", offs_sb)
        xb = pick_words("xb", two_sb)

        def interleave(dst, src):
            nc.scalar.copy(
                dst.rearrange("p (c i j) -> p c j i", i=2, j=PACK), src.rearrange("p j (c i) -> p c j i", i=2)
            )

        def quantize(codes, scales, values):
            nc.vector.quantize_mx(out=codes.bitcast(FP8X4), scales=scales, in_=values)

        def product(name, lhs, lhs_scales, rhs, rhs_scales):
            acc = psum.tile([P, rhs.shape[1]], F32, name=name, tag="product", bufs=PRODUCT_BANKS)
            nc.tensor.matmul_mx(
                out=acc[:],
                lhsT=lhs.bitcast(FP8X4),
                lhsT_scale=lhs_scales,
                rhs=rhs.bitcast(FP8X4),
                rhs_scale=rhs_scales,
                start=True,
                stop=True,
            )
            return acc

        wa_codes = keep.tile([P, H], U32, name="wa_codes", align_bytes=ALIGN)
        wa_scales = keep.tile([P, H], U8, name="wa_scales", align_bytes=ALIGN)
        for half in range(2):
            wa_grouped = keep.tile([P, HALF * PACK], BF16, name=f"wa_grouped{half}", align_bytes=ALIGN)
            interleave(wa_grouped[:], wa_raw[half][:])
            cols = slice(half * HALF, (half + 1) * HALF)
            quantize(wa_codes[:, cols], wa_scales[:, cols], wa_grouped[:])
        a = []
        for t in range(PACK):
            tokens = slice(t * P, (t + 1) * P)
            acc = product(f"a_ps{t}", xa[:, tokens], xa_scales[:, tokens], wa_codes[:], wa_scales[:])
            a.append(keep.tile([P, H], F32, name=f"a{t}"))
            nc.scalar.copy(a[t][:], acc[:])

        def fetch_old(u, dst):
            nc.vector.tensor_copy(dst, page[u][:].indirect(n3_sb[:]))

        old0 = keep.tile([P, N], F32, name="old0")
        fetch_old(0, old0[:])

        pa, pb = [], []
        for t in range(PACK):
            pa.append(keep.tile([P, W], F32, name=f"pa{t}"))
            pb.append(keep.tile([P, W], F32, name=f"pb{t}"))
            nc.vector.tensor_copy(pa[t][:], a[t][:].indirect(n1_sb[:]))
            nc.vector.tensor_copy(pb[t][:], a[t][:].indirect(n2_sb[:]))

        wb_grouped = keep.tile([P, N * PACK], BF16, name="wb_grouped", align_bytes=ALIGN)
        interleave(wb_grouped[:], wb_raw[:])
        wb_codes = keep.tile([P, N], U32, name="wb_codes", align_bytes=ALIGN)
        wb_scales = keep.tile([P, N], U8, name="wb_scales", align_bytes=ALIGN)
        quantize(wb_codes[:], wb_scales[:], wb_grouped[:])
        z2_rows = keep.tile([P, PACK, N], BF16, name="z2_rows")
        for t in range(PACK):
            tokens = slice(t * P, (t + 1) * P)
            acc = product(f"b_ps{t}", xb[:, tokens], xb_scales[:, tokens], wb_codes[:], wb_scales[:])
            nc.scalar.activation(z2_rows[:, t, :], acc[:], COPY, scale=gates[:, PACK + t : PACK + t + 1])
        z2_grouped = keep.tile([P, N * PACK], BF16, name="z2_grouped", align_bytes=ALIGN)
        interleave(z2_grouped[:], z2_rows[:])

        dt = [keep.tile([P, H], F32, name="dt0")]
        for t in range(1, PACK):
            dt.append(reuse.tile([P, H], F32, name=f"dt{t}", offset=(t - 1) * H * 4))
        z_rows = [keep.tile([P, PACK, P, 2], BF16, name=f"z_rows{half}") for half in range(2)]
        z_grouped = [
            keep.tile([P, 2, P, PACK], BF16, name=f"z_grouped{half}", align_bytes=ALIGN) for half in range(2)
        ]

        def put_sum(t):
            nc.vector.tensor_tensor(dt[t][:].indirect(n1_sb[:]), pa[t][:], pb[t][:], ADD)

        def put_product(t):
            nc.vector.tensor_tensor(dt[t][:].indirect(n2_sb[:]), pa[t][:], pb[t][:], MULT)

        def weigh(t, half):
            cols = dt[t][:].rearrange("p (m u) -> p m u", u=PACK)[:, :, 2 * half : 2 * half + 2]
            nc.scalar.activation(z_rows[half][:, t], cols, COPY, scale=gates[:, t : t + 1])

        put_sum(0)
        for t in range(PACK):
            if t + 1 < PACK:
                put_sum(t + 1)
            put_product(t)
        for t in range(PACK - 1):
            for half in range(2):
                weigh(t, half)
        for half in range(2):
            weigh(PACK - 1, half)
            nc.scalar.copy(z_grouped[half][:], z_rows[half][:].rearrange("p t m e -> p e m t"))

        old12 = keep.tile([P, 2, N], F32, name="old12", tag="pa2")
        for e in range(2):
            fetch_old(1 + e, old12[:, e, :])
        z2_codes = keep.tile([P, N], U32, name="z2_codes", align_bytes=ALIGN)
        z2_scales = keep.tile([P, N], U8, name="z2_scales", align_bytes=ALIGN)
        quantize(z2_codes[:], z2_scales[:], z2_grouped[:])
        z_codes = keep.tile([P, H], U32, name="z_codes", align_bytes=ALIGN)
        z_scales = keep.tile([P, H], U8, name="z_scales", align_bytes=ALIGN)
        cv = keep.tile([P, PACK, N], F32, name="cv")
        for half in range(2):
            cols = slice(half * HALF, (half + 1) * HALF)
            quantize(z_codes[:, cols], z_scales[:, cols], z_grouped[half][:].rearrange("p e m t -> p (e m t)"))
            for u in range(2 * half, 2 * half + 2):
                rows = slice(u * P, (u + 1) * P)
                acc = product(f"cv_ps{u}", z_codes[:, rows], z_scales[:, rows], z2_codes[:], z2_scales[:])
                nc.scalar.activation(cv[:, u, :], acc[:], COPY, scale=0.0625)
        old3 = keep.tile([P, N], F32, name="old3", tag="z_rows0")
        fetch_old(3, old3[:])
        nw = keep.tile([P, PACK, N], F32, name="nw")
        nc.vector.scalar_tensor_tensor(nw[:, 0, :], old0[:], 0.5, cv[:, 0, :], MULT, MAX)
        nc.vector.scalar_tensor_tensor(nw[:, 1:3, :], old12[:], 0.5, cv[:, 1:3, :], MULT, MAX)
        nc.vector.scalar_tensor_tensor(nw[:, 3, :], old3[:], 0.5, cv[:, 3, :], MULT, MAX)
        for u in range(PACK):
            nc.vector.tensor_copy(page[u][:].indirect(n3_sb[:]), nw[:, u, :])
            nc.sync.dma_start(out_rows[u], page[u][:])
